import numpy as np
import ml_dtypes


def mxq(x, axis, fmt="e4m3"):
    dtype, down = {"e4m3": (ml_dtypes.float8_e4m3fn, 7), "e5m2": (ml_dtypes.float8_e5m2, 14)}[fmt]
    v = np.moveaxis(np.asarray(x, np.float32).astype(ml_dtypes.bfloat16).astype(np.float64), axis, -1)
    blocks = v.reshape(v.shape[:-1] + (-1, 32))
    amax = np.abs(blocks).max(-1, keepdims=True)
    byte = np.maximum(np.where(amax > 0, np.frexp(amax)[1] - 1 + 127, 0) - down, 1)
    scale = np.exp2(byte - 127.0)
    codes = (blocks / scale).astype(np.float32).astype(dtype).astype(np.float64)
    return np.moveaxis((codes * scale).reshape(v.shape), -1, axis)


WIDE = False


def mx_kscale(k):
    if not WIDE:
        return np.ones(k)
    levels = np.array([10, -10, 5, -5, 0])
    if k % 512:
        return np.exp2(np.random.permutation(np.resize(levels, k // 32))).repeat(32)
    a = np.empty((k // 512, 16))
    for p in range(k // 512):
        a[p, :8] = np.random.permutation(np.resize(levels, 8))
        for g in range(8):
            far = levels[np.abs(levels - a[p, g]) >= 10]
            a[p, g + 8] = far[np.random.randint(len(far))]
    return np.exp2(a.ravel()).repeat(32)


def f64(x):
    return np.asarray(x).astype(np.float64)


def striped(idx):
    return np.tile(idx.reshape(-1, 16).T, (8, 1)).astype(np.uint16)


def unstriped(offs):
    return offs[:16].T.reshape(-1).astype(np.int64)


def gelu(v):
    return 0.5 * v * (1.0 + np.tanh(np.sqrt(2.0 / np.pi) * (v + 0.044715 * v**3)))


K, T, E, C, H, N = 512, 768, 4, 128, 1024, 256


def by_expert(wq, xq):
    return np.concatenate([wq[e].T @ xq[:, e * C:(e + 1) * C] for e in range(E)], axis=1)


def setup_inputs():
    n = np.random.standard_normal
    s = mx_kscale(K)[:, None]
    u = mx_kscale(H)
    return {
        "xT": (n((K, T)) * s).astype(np.float32),
        "w1": (n((E + 1, K, H)) / np.sqrt(K) / s[None] * u[None, None, :]).astype(np.float32),
        "w2": (n((E + 1, H, N)) / np.sqrt(H) / u[None, :, None]).astype(np.float32),
        "gate": np.tile(np.random.uniform(0.2, 1.0, E * C), (N, 1)).astype(np.float32),
        "offs": striped(np.random.permutation(T)[:E * C]),
    }


def reference(xT, w1, w2, gate, offs):
    idx = unstriped(offs)
    w1q, w2q = mxq(f64(w1), 1, "e4m3"), mxq(f64(w2), 1, "e4m3")
    xs = mxq(f64(xT), 0, "e4m3")
    hs = gelu(w1q[E].T @ xs)
    ys = w2q[E].T @ mxq(hs, 0, "e4m3")
    xq = mxq(f64(xT)[:, idx], 0, "e4m3")
    h = gelu(by_expert(w1q, xq))
    y = by_expert(w2q, mxq(h, 0, "e4m3"))
    out = ys
    out[:, idx] += f64(gate) * y
    return out

@@ -1,0 +1,291 @@
+from contextlib import ExitStack
+
+import concourse.mybir as mybir
+
+K, T, E, C, H, N = 512, 768, 4, 128, 1024, 256
+S = E * C
+FLOPS = 2 * (T + S) * (K * H + H * N)
+
+F32 = mybir.dt.float32
+BF16 = mybir.dt.bfloat16
+U32 = mybir.dt.uint32
+U16 = mybir.dt.uint16
+U8 = mybir.dt.uint8
+FP8X4 = mybir.dt.float8_e4m3fn_x4
+ADD = mybir.AluOpType.add
+MULT = mybir.AluOpType.mult
+GELU = mybir.ActivationFunctionType.Gelu_apprx_tanh
+
+P = 128
+PACK = 4
+SHARED = E
+
+TOKEN_CUTS = ((0, 256), (256, 768))
+V_W1 = {0: (64, 128), 1: (128, 32), 2: (48, 64), 3: (64, 48), SHARED: (16, 128)}
+V_LAST = (224, 96)
+
+
+def tile_moe_shr_mlp_gelu_kernel(tc, xT, w1, w2, gate, offs, out):
+    nc = tc.nc
+
+    with ExitStack() as ctx:
+        held = ctx.enter_context(tc.tile_pool(name="held", bufs=1))
+        work = ctx.enter_context(tc.tile_pool(name="work", bufs=2))
+        psum = ctx.enter_context(tc.psum_pool(name="psum", bufs=8))
+
+        def on_vector(dst, src):
+            nc.vector.tensor_copy(out=dst, in_=src)
+
+        def on_scalar(dst, src):
+            nc.scalar.copy(out=dst, in_=src)
+
+        def held_codes(width, name):
+            codes = held.tile([P, width], U32, name=name + "_codes", align_bytes=64)
+            scales = held.tile([P, width], U8, name=name + "_scales", align_bytes=64)
+            return codes, scales
+
+        def quantize(q, cols, values):
+            nc.vector.quantize_mx(out=q[0][:, cols].bitcast(FP8X4), scales=q[1][:, cols], in_=values)
+
+        def multiply(bank, w_q, w_col, x_q, x_cols, start, stop):
+            w_cols = slice(w_col, w_col + P)
+            nc.tensor.matmul_mx(
+                out=bank,
+                lhsT=w_q[0][:, w_cols].bitcast(FP8X4),
+                lhsT_scale=w_q[1][:, w_cols],
+                rhs=x_q[0][:, x_cols].bitcast(FP8X4),
+                rhs_scale=x_q[1][:, x_cols],
+                start=start,
+                stop=stop,
+            )
+
+        x_rows = xT.rearrange("(p j) t -> p j t", j=PACK)
+        x_raw = []
+        offsets = held.tile([P, S // 16], U16, name="offsets")
+        for a, b in TOKEN_CUTS:
+            piece = held.tile([P, PACK, b - a], F32, name=f"x_raw{a}")
+            nc.sync.dma_start(out=piece[:], in_=x_rows[:, :, a:b])
+            x_raw.append(piece)
+            if a == 0:
+                nc.sync.dma_start(offsets[:], offs)
+        gates = held.tile([P, S], F32, name="gates")
+
+        def load_w1(e, g):
+            raw = work.tile([P, 2048], F32, name="raw", tag="raw", bufs=10)
+            nc.sync.dma_start(
+                out=raw[:].rearrange("p (j c) -> p j c", j=PACK),
+                in_=w1[e].rearrange("(p j) c -> p j c", j=PACK)[:, :, g * 512 : (g + 1) * 512],
+            )
+            return raw
+
+        raw1 = {}
+        raw2 = {}
+        for g in range(2):
+            raw1[SHARED, g] = load_w1(SHARED, g)
+        for e in range(E):
+            for g in range(2):
+                raw1[e, g] = load_w1(e, g)
+            if e == 0:
+                nc.sync.dma_start(out=gates[:], in_=gate[0:P, :])
+            raw = work.tile([P, 2048], F32, name="raw", tag="raw", bufs=10)
+            nc.sync.dma_start(
+                out=raw[:].rearrange("p (g j n) -> p g j n", g=2, j=PACK),
+                in_=w2[e].rearrange("(g p j) n -> p g j n", g=2, j=PACK),
+            )
+            raw2[e] = raw
+        for g in range(2):
+            last = held.tile([P, 1024], F32, name=f"last_raw{g}")
+            nc.sync.dma_start(
+                out=last[:].rearrange("p (j n) -> p j n", j=PACK),
+                in_=w2[SHARED].rearrange("(g p j) n -> p g j n", g=2, j=PACK)[:, g, :, :],
+            )
+            raw2[SHARED, g] = last
+
+        warm = held.tile([P, 1], F32, name="warm")
+        nc.gpsimd.memset(warm[:], 0.0)
+        warm_out = held.tile([P, 1], F32, name="warm_out")
+        nc.scalar.activation(out=warm_out[:], in_=warm[:], func=GELU)
+        routed = []
+        for h in range(2):
+            window = held.tile([P, T], F32, name=f"routed{h}")
+            nc.gpsimd.memset(window[:], 0.0)
+            routed.append(window)
+
+        pairs = [held.tile([P, 2 * T], BF16, name=f"pairs{u}", align_bytes=64) for u in range(2)]
+        x_bf = held.tile([P, PACK * T], BF16, name="x_bf", align_bytes=64)
+        x_q = held_codes(T, "x")
+        slots_bf = held.tile([P, PACK * S], BF16, name="slots_bf", align_bytes=64)
+        slots_q = held_codes(S, "slot")
+
+        def pair_plane(copy, piece, u, a, b):
+            copy(
+                pairs[u][:, 2 * a : 2 * b].rearrange("p (c i k) -> p c k i", i=4, k=2),
+                piece[:, 2 * u : 2 * u + 2, :].rearrange("p k (c i) -> p c k i", i=4),
+            )
+
+        def interleave_tokens(copy, piece, a, b):
+            copy(
+                x_bf[:, PACK * a : PACK * b].rearrange("p (c i j) -> p c j i", i=4, j=PACK),
+                piece.rearrange("p j (c i) -> p c j i", i=4),
+            )
+
+        pair_plane(on_vector, x_raw[0], 0, 0, 256)
+        pair_plane(on_vector, x_raw[0], 1, 0, 256)
+        interleave_tokens(on_scalar, x_raw[0][:], 0, 256)
+        pair_plane(on_vector, x_raw[1], 0, 256, 768)
+        pair_plane(on_scalar, x_raw[1], 1, 256, 768)
+        interleave_tokens(on_vector, x_raw[1][:, :, 0:256], 256, 512)
+        interleave_tokens(on_scalar, x_raw[1][:, :, 256:512], 512, 768)
+        quantize(x_q, slice(0, 256), x_bf[:, 0:1024])
+        quantize(x_q, slice(256, 768), x_bf[:, 1024:3072])
+
+        def gather(u):
+            nc.vector.tensor_copy(
+                slots_bf[:].bitcast(U32).rearrange("p (s u) -> p s u", u=2)[:, :, u],
+                pairs[u][:].bitcast(U32).indirect(offsets[:]),
+            )
+
+        def quantize_w(w_bf):
+            codes = work.tile([P, 512], U32, name="w_codes", tag="w_codes", bufs=8, align_bytes=64)
+            scales = work.tile([P, 512], U8, name="w_scales", tag="w_scales", bufs=8, align_bytes=64)
+            quantize((codes, scales), slice(0, 512), w_bf[:])
+            return codes, scales
+
+        def interleave_w1(e, g):
+            w_bf = work.tile([P, 2048], BF16, name="w_bf", tag="w_bf", bufs=6, align_bytes=64)
+            dst = w_bf[:].rearrange("p (t m j) -> p m j t", t=4, j=PACK)
+            src = raw1[e, g][:].rearrange("p (j m t) -> p m j t", j=PACK, t=4)
+            cut = V_W1[e][g]
+            if cut > 0:
+                on_vector(dst[:, 0:cut], src[:, 0:cut])
+            if cut < P:
+                on_scalar(dst[:, cut:P], src[:, cut:P])
+            return w_bf
+
+        def interleave_rows(copy, w_bf, raw):
+            copy(
+                w_bf.rearrange("p (c i j) -> p c j i", i=4, j=PACK),
+                raw.rearrange("p j (c i) -> p c j i", i=4),
+            )
+
+        def interleave_w2(e):
+            w_bf = work.tile([P, 2048], BF16, name="w_bf", tag="w_bf", bufs=6, align_bytes=64)
+            rows = raw2[e][:].rearrange("p (g j n) -> p g j n", g=2, j=PACK)
+            interleave_rows(on_vector, w_bf[:, 0:1024], rows[:, 0])
+            interleave_rows(on_scalar, w_bf[:, 1024:2048], rows[:, 1])
+            return w_bf
+
+        def hidden(w_q, x, x_col, h_bf):
+            bank = psum.tile([P, 4, P], F32, name="bank", tag="bank")
+            for t in range(4):
+                multiply(bank[:, t, :], w_q, t * P, x, slice(x_col, x_col + P), True, True)
+            nc.scalar.activation(
+                out=h_bf.rearrange("p (n t) -> p n t", t=4),
+                in_=bank[:].rearrange("p t n -> p n t"),
+                func=GELU,
+            )
+
+        shared_bf = [held.tile([P, PACK * T], BF16, name=f"hs_bf{g}", align_bytes=64) for g in range(2)]
+        shared_q = [held_codes(T, f"hs{g}") for g in range(2)]
+
+        def hidden_shared(w_q, g, blocks):
+            for b in blocks:
+                hidden(w_q, x_q, b * P, shared_bf[g][:, b * 512 : (b + 1) * 512])
+
+        def quantize_shared(g):
+            quantize(shared_q[g], slice(0, 512), shared_bf[g][:, 0:2048])
+            quantize(shared_q[g], slice(512, 768), shared_bf[g][:, 2048:3072])
+
+        def hidden_routed(w_q, e, g, h_bf):
+            hidden(w_q, slots_q, e * C, h_bf[:, g * 512 : (g + 1) * 512])
+
+        def new_h():
+            return work.tile([P, H], BF16, name="h_bf", tag="h_bf", bufs=3, align_bytes=64)
+
+        def second_layer(e, h_bf, w2_bf):
+            h_codes = work.tile([P, 2 * C], U32, name="h_codes", tag="h_codes", bufs=3, align_bytes=64)
+            h_scales = work.tile([P, 2 * C], U8, name="h_scales", tag="h_scales", bufs=3, align_bytes=64)
+            h_q = (h_codes, h_scales)
+            quantize(h_q, slice(0, 2 * C), h_bf[:])
+            w2_q = quantize_w(w2_bf)
+            y = psum.tile([P, 2, C], F32, name="bank", tag="bank")
+            for h in range(2):
+                for g in range(2):
+                    multiply(y[:, h, :], w2_q, g * N + h * P, h_q, slice(g * C, (g + 1) * C), g == 0, g == 1)
+            y_sb = work.tile([P, 2 * C], F32, name="y_sb", tag="y_sb", bufs=3)
+            nc.scalar.copy(out=y_sb[:], in_=y[:].rearrange("p h c -> p (h c)"))
+            return y_sb
+
+        def scatter(e, h, y_sb):
+            nc.vector.tensor_tensor(
+                routed[h][:].indirect(offsets[:, e * C // 16 : (e + 1) * C // 16]),
+                y_sb[:, h * C : (h + 1) * C],
+                gates[:, e * C : (e + 1) * C],
+                MULT,
+            )
+
+        w_bf = interleave_w1(SHARED, 0)
+        gather(0)
+        w_q = quantize_w(w_bf)
+        gather(1)
+        hidden_shared(w_q, 0, range(6))
+        w_bf = interleave_w1(SHARED, 1)
+        quantize(slots_q, slice(0, S), slots_bf[:])
+        ws_q = quantize_w(w_bf)
+
+        y_sb = None
+        for e in range(E):
+            w_bf0 = interleave_w1(e, 0)
+            if e == 0:
+                hidden_shared(ws_q, 1, range(3))
+            else:
+                y_sb = second_layer(e - 1, h_bf, w2_bf)
+            w_bf1 = interleave_w1(e, 1)
+            h_bf = new_h()
+            hidden_routed(quantize_w(w_bf0), e, 0, h_bf)
+            if e < 2:
+                quantize_shared(e)
+            if e > 0:
+                scatter(e - 1, 0, y_sb)
+                hidden_routed(quantize_w(w_bf1), e, 1, h_bf)
+                w2_bf = interleave_w2(e)
+                scatter(e - 1, 1, y_sb)
+            else:
+                w2_bf = interleave_w2(e)
+                hidden_routed(quantize_w(w_bf1), e, 1, h_bf)
+                hidden_shared(ws_q, 1, range(3, 6))
+
+        blocks = ((512, 768), (0, 512))
+        banks = {}
+        for h in range(2):
+            for a, b in blocks:
+                banks[h, a] = psum.tile([P, b - a], F32, name="bank", tag="bank")
+
+        last_bf = [held.tile([P, 1024], BF16, name=f"last_bf{g}", align_bytes=64) for g in range(2)]
+        last_q = [held_codes(N, f"last{g}") for g in range(2)]
+
+        def interleave_last(g):
+            rows = raw2[SHARED, g][:].rearrange("p (j n) -> p j n", j=PACK)
+            cut = V_LAST[g]
+            interleave_rows(on_vector, last_bf[g][:, 0 : PACK * cut], rows[:, :, 0:cut])
+            interleave_rows(on_scalar, last_bf[g][:, PACK * cut : PACK * N], rows[:, :, cut:N])
+
+        def multiply_last(g):
+            for h in range(2):
+                for a, b in blocks:
+                    multiply(banks[h, a][:], last_q[g], h * P, shared_q[g], slice(a, b), g == 0, g == 1)
+
+        interleave_last(0)
+        y_sb = second_layer(E - 1, h_bf, w2_bf)
+        quantize(last_q[0], slice(0, N), last_bf[0][:])
+        interleave_last(1)
+        multiply_last(0)
+        scatter(E - 1, 0, y_sb)
+        quantize(last_q[1], slice(0, N), last_bf[1][:])
+        multiply_last(1)
+        scatter(E - 1, 1, y_sb)
+        for h in range(2):
+            for a, b in blocks:
+                result = held.tile([P, b - a], F32, name=f"result{h}_{a}")
+                nc.vector.tensor_tensor(result[:], banks[h, a][:], routed[h][:, a:b], ADD)
+                nc.sync.dma_start(out=out[h * P : (h + 1) * P, a:b], in_=result[:])

@@ -21,8 +21,15 @@ PACK = 4
 SHARED = E
 
 TOKEN_CUTS = ((0, 256), (256, 768))
-V_W1 = {0: (64, 128), 1: (128, 32), 2: (48, 64), 3: (64, 48), SHARED: (16, 128)}
-V_LAST = (224, 96)
+SCALAR, VECTOR, VECTOR_HALVES, SCALAR_HALVES, VECTOR_SCALAR = range(5)
+W1_COPY = {
+    SHARED: (SCALAR, VECTOR_HALVES),
+    0: (VECTOR_HALVES, VECTOR_HALVES),
+    1: (VECTOR_HALVES, SCALAR),
+    2: (VECTOR, SCALAR),
+    3: (VECTOR, SCALAR_HALVES),
+}
+W2_COPY = {0: VECTOR_HALVES, 1: VECTOR_HALVES, 2: VECTOR_HALVES, 3: VECTOR_SCALAR}
 
 
 def tile_moe_shr_mlp_gelu_kernel(tc, xT, w1, w2, gate, offs, out):
@@ -62,16 +69,16 @@ def tile_moe_shr_mlp_gelu_kernel(tc, xT, w1, w2, gate, offs, out):
         x_rows = xT.rearrange("(p j) t -> p j t", j=PACK)
         x_raw = []
         offsets = held.tile([P, S // 16], U16, name="offsets")
-        for a, b in TOKEN_CUTS:
+
+        def load_tokens(a, b):
             piece = held.tile([P, PACK, b - a], F32, name=f"x_raw{a}")
             nc.sync.dma_start(out=piece[:], in_=x_rows[:, :, a:b])
             x_raw.append(piece)
-            if a == 0:
-                nc.sync.dma_start(offsets[:], offs)
+
         gates = held.tile([P, S], F32, name="gates")
 
         def load_w1(e, g):
-            raw = work.tile([P, 2048], F32, name="raw", tag="raw", bufs=10)
+            raw = work.tile([P, 2048], F32, name="raw", tag="raw", bufs=7)
             nc.sync.dma_start(
                 out=raw[:].rearrange("p (j c) -> p j c", j=PACK),
                 in_=w1[e].rearrange("(p j) c -> p j c", j=PACK)[:, :, g * 512 : (g + 1) * 512],
@@ -80,26 +87,29 @@ def tile_moe_shr_mlp_gelu_kernel(tc, xT, w1, w2, gate, offs, out):
 
         raw1 = {}
         raw2 = {}
-        for g in range(2):
-            raw1[SHARED, g] = load_w1(SHARED, g)
+        load_tokens(0, 256)
+        nc.sync.dma_start(offsets[:], offs)
+        load_tokens(256, 768)
+        raw1[SHARED, 0] = load_w1(SHARED, 0)
+        raw1[SHARED, 1] = load_w1(SHARED, 1)
         for e in range(E):
             for g in range(2):
                 raw1[e, g] = load_w1(e, g)
             if e == 0:
                 nc.sync.dma_start(out=gates[:], in_=gate[0:P, :])
-            raw = work.tile([P, 2048], F32, name="raw", tag="raw", bufs=10)
+            raw = work.tile([P, 2048], F32, name="raw", tag="raw", bufs=7)
             nc.sync.dma_start(
                 out=raw[:].rearrange("p (g j n) -> p g j n", g=2, j=PACK),
                 in_=w2[e].rearrange("(g p j) n -> p g j n", g=2, j=PACK),
             )
             raw2[e] = raw
-        for g in range(2):
-            last = held.tile([P, 1024], F32, name=f"last_raw{g}")
-            nc.sync.dma_start(
-                out=last[:].rearrange("p (j n) -> p j n", j=PACK),
-                in_=w2[SHARED].rearrange("(g p j) n -> p g j n", g=2, j=PACK)[:, g, :, :],
-            )
-            raw2[SHARED, g] = last
+        last_rows = w2[SHARED].rearrange("(g p j) n -> p g j n", g=2, j=PACK)
+        last_parts = ((0, 0, N), (1, 0, P), (1, P, N))
+        last_raw = []
+        for g, a, b in last_parts:
+            last = held.tile([P, PACK, b - a], F32, name=f"last_raw{g}_{a}")
+            nc.sync.dma_start(out=last[:], in_=last_rows[:, g, :, a:b])
+            last_raw.append(last)
 
         warm = held.tile([P, 1], F32, name="warm")
         nc.gpsimd.memset(warm[:], 0.0)
@@ -129,38 +139,39 @@ def tile_moe_shr_mlp_gelu_kernel(tc, xT, w1, w2, gate, offs, out):
                 piece.rearrange("p j (c i) -> p c j i", i=4),
             )
 
-        pair_plane(on_vector, x_raw[0], 0, 0, 256)
-        pair_plane(on_vector, x_raw[0], 1, 0, 256)
-        interleave_tokens(on_scalar, x_raw[0][:], 0, 256)
-        pair_plane(on_vector, x_raw[1], 0, 256, 768)
-        pair_plane(on_scalar, x_raw[1], 1, 256, 768)
-        interleave_tokens(on_vector, x_raw[1][:, :, 0:256], 256, 512)
-        interleave_tokens(on_scalar, x_raw[1][:, :, 256:512], 512, 768)
-        quantize(x_q, slice(0, 256), x_bf[:, 0:1024])
-        quantize(x_q, slice(256, 768), x_bf[:, 1024:3072])
-
         def gather(u):
             nc.vector.tensor_copy(
                 slots_bf[:].bitcast(U32).rearrange("p (s u) -> p s u", u=2)[:, :, u],
                 pairs[u][:].bitcast(U32).indirect(offsets[:]),
             )
 
-        def quantize_w(w_bf):
-            codes = work.tile([P, 512], U32, name="w_codes", tag="w_codes", bufs=8, align_bytes=64)
-            scales = work.tile([P, 512], U8, name="w_scales", tag="w_scales", bufs=8, align_bytes=64)
-            quantize((codes, scales), slice(0, 512), w_bf[:])
+        def engines(choice):
+            return {
+                VECTOR: (on_vector,),
+                SCALAR: (on_scalar,),
+                VECTOR_HALVES: (on_vector, on_vector),
+                SCALAR_HALVES: (on_scalar, on_scalar),
+                VECTOR_SCALAR: (on_vector, on_scalar),
+            }[choice]
+
+        def quantize_w(w_bf, parts):
+            codes = work.tile([P, 512], U32, name="w_codes", tag="w_codes", bufs=14, align_bytes=64)
+            scales = work.tile([P, 512], U8, name="w_scales", tag="w_scales", bufs=14, align_bytes=64)
+            step = 512 // parts
+            for i in range(parts):
+                quantize((codes, scales), slice(i * step, (i + 1) * step), w_bf[:, PACK * i * step : PACK * (i + 1) * step])
             return codes, scales
 
         def interleave_w1(e, g):
-            w_bf = work.tile([P, 2048], BF16, name="w_bf", tag="w_bf", bufs=6, align_bytes=64)
+            w_bf = work.tile([P, 2048], BF16, name="w_bf", tag="w_bf", bufs=7, align_bytes=64)
             dst = w_bf[:].rearrange("p (t m j) -> p m j t", t=4, j=PACK)
             src = raw1[e, g][:].rearrange("p (j m t) -> p m j t", j=PACK, t=4)
-            cut = V_W1[e][g]
-            if cut > 0:
-                on_vector(dst[:, 0:cut], src[:, 0:cut])
-            if cut < P:
-                on_scalar(dst[:, cut:P], src[:, cut:P])
-            return w_bf
+            copies = engines(W1_COPY[e][g])
+            step = 4 // len(copies)
+            for i, copy in enumerate(copies):
+                t = slice(i * step, (i + 1) * step)
+                copy(dst[:, :, :, t], src[:, :, :, t])
+            return w_bf, len(copies)
 
         def interleave_rows(copy, w_bf, raw):
             copy(
@@ -169,11 +180,12 @@ def tile_moe_shr_mlp_gelu_kernel(tc, xT, w1, w2, gate, offs, out):
             )
 
         def interleave_w2(e):
-            w_bf = work.tile([P, 2048], BF16, name="w_bf", tag="w_bf", bufs=6, align_bytes=64)
+            w_bf = work.tile([P, 2048], BF16, name="w_bf", tag="w_bf", bufs=7, align_bytes=64)
             rows = raw2[e][:].rearrange("p (g j n) -> p g j n", g=2, j=PACK)
-            interleave_rows(on_vector, w_bf[:, 0:1024], rows[:, 0])
-            interleave_rows(on_scalar, w_bf[:, 1024:2048], rows[:, 1])
-            return w_bf
+            copies = engines(W2_COPY[e])
+            for i, copy in enumerate(copies):
+                interleave_rows(copy, w_bf[:, 1024 * i : 1024 * (i + 1)], rows[:, i])
+            return w_bf, len(copies)
 
         def hidden(w_q, x, x_col, h_bf):
             bank = psum.tile([P, 4, P], F32, name="bank", tag="bank")
@@ -188,8 +200,8 @@ def tile_moe_shr_mlp_gelu_kernel(tc, xT, w1, w2, gate, offs, out):
         shared_bf = [held.tile([P, PACK * T], BF16, name=f"hs_bf{g}", align_bytes=64) for g in range(2)]
         shared_q = [held_codes(T, f"hs{g}") for g in range(2)]
 
-        def hidden_shared(w_q, g, blocks):
-            for b in blocks:
+        def hidden_shared(w_q, g):
+            for b in range(T // P):
                 hidden(w_q, x_q, b * P, shared_bf[g][:, b * 512 : (b + 1) * 512])
 
         def quantize_shared(g):
@@ -200,90 +212,91 @@ def tile_moe_shr_mlp_gelu_kernel(tc, xT, w1, w2, gate, offs, out):
             hidden(w_q, slots_q, e * C, h_bf[:, g * 512 : (g + 1) * 512])
 
         def new_h():
-            return work.tile([P, H], BF16, name="h_bf", tag="h_bf", bufs=3, align_bytes=64)
+            return work.tile([P, H], BF16, name="h_bf", tag="h_bf", bufs=4, align_bytes=64)
 
-        def second_layer(e, h_bf, w2_bf):
-            h_codes = work.tile([P, 2 * C], U32, name="h_codes", tag="h_codes", bufs=3, align_bytes=64)
-            h_scales = work.tile([P, 2 * C], U8, name="h_scales", tag="h_scales", bufs=3, align_bytes=64)
+        def second_layer(e, h_bf, w2_q):
+            h_codes = work.tile([P, 2 * C], U32, name="h_codes", tag="h_codes", bufs=4, align_bytes=64)
+            h_scales = work.tile([P, 2 * C], U8, name="h_scales", tag="h_scales", bufs=4, align_bytes=64)
             h_q = (h_codes, h_scales)
             quantize(h_q, slice(0, 2 * C), h_bf[:])
-            w2_q = quantize_w(w2_bf)
             y = psum.tile([P, 2, C], F32, name="bank", tag="bank")
             for h in range(2):
                 for g in range(2):
                     multiply(y[:, h, :], w2_q, g * N + h * P, h_q, slice(g * C, (g + 1) * C), g == 0, g == 1)
-            y_sb = work.tile([P, 2 * C], F32, name="y_sb", tag="y_sb", bufs=3)
-            nc.scalar.copy(out=y_sb[:], in_=y[:].rearrange("p h c -> p (h c)"))
+            y_sb = work.tile([P, 2, C], F32, name="y_sb", tag="y_sb", bufs=4)
+            for h in range(2):
+                nc.vector.tensor_tensor(y_sb[:, h, :], y[:, h, :], gates[:, e * C : (e + 1) * C], MULT)
             return y_sb
 
         def scatter(e, h, y_sb):
-            nc.vector.tensor_tensor(
-                routed[h][:].indirect(offsets[:, e * C // 16 : (e + 1) * C // 16]),
-                y_sb[:, h * C : (h + 1) * C],
-                gates[:, e * C : (e + 1) * C],
-                MULT,
-            )
+            nc.vector.tensor_copy(routed[h][:].indirect(offsets[:, e * C // 16 : (e + 1) * C // 16]), y_sb[:, h, :])
 
-        w_bf = interleave_w1(SHARED, 0)
+        last_bf = [held.tile([P, PACK * (b - a)], BF16, name=f"last_bf{g}_{a}", align_bytes=64) for g, a, b in last_parts]
+        last_q = [held_codes(N, f"last{g}") for g in range(2)]
+
+        def interleave_last(i):
+            width = last_raw[i].shape[2]
+            cut = width // 2
+            interleave_rows(on_vector, last_bf[i][:, 0 : PACK * cut], last_raw[i][:, :, 0:cut])
+            interleave_rows(on_scalar, last_bf[i][:, PACK * cut : PACK * width], last_raw[i][:, :, cut:width])
+
+        pair_plane(on_vector, x_raw[0][:], 0, 0, 256)
+        pair_plane(on_scalar, x_raw[0][:], 1, 0, 256)
+        interleave_tokens(on_scalar, x_raw[0][:], 0, 256)
+        pair_plane(on_vector, x_raw[1][:], 0, 256, 768)
+        pair_plane(on_scalar, x_raw[1][:], 1, 256, 768)
+        interleave_tokens(on_vector, x_raw[1][:, :, 0:256], 256, 512)
+        interleave_tokens(on_scalar, x_raw[1][:, :, 256:512], 512, 768)
+
+        w1_bf = {}
+        w2_bf = {}
+        for e in [SHARED] + list(range(E)):
+            for g in range(2):
+                w1_bf[e, g] = interleave_w1(e, g)
+            if e != SHARED:
+                w2_bf[e] = interleave_w2(e)
+        for i in range(3):
+            interleave_last(i)
+
+        quantize(x_q, slice(0, 256), x_bf[:, 0:1024])
+        quantize(x_q, slice(256, 768), x_bf[:, 1024:3072])
+        w1_q = {}
+        w2_q = {}
+        w1_q[SHARED, 0] = quantize_w(*w1_bf[SHARED, 0])
         gather(0)
-        w_q = quantize_w(w_bf)
         gather(1)
-        hidden_shared(w_q, 0, range(6))
-        w_bf = interleave_w1(SHARED, 1)
+        w1_q[SHARED, 1] = quantize_w(*w1_bf[SHARED, 1])
         quantize(slots_q, slice(0, S), slots_bf[:])
-        ws_q = quantize_w(w_bf)
-
-        y_sb = None
         for e in range(E):
-            w_bf0 = interleave_w1(e, 0)
-            if e == 0:
-                hidden_shared(ws_q, 1, range(3))
-            else:
-                y_sb = second_layer(e - 1, h_bf, w2_bf)
-            w_bf1 = interleave_w1(e, 1)
-            h_bf = new_h()
-            hidden_routed(quantize_w(w_bf0), e, 0, h_bf)
-            if e < 2:
-                quantize_shared(e)
-            if e > 0:
-                scatter(e - 1, 0, y_sb)
-                hidden_routed(quantize_w(w_bf1), e, 1, h_bf)
-                w2_bf = interleave_w2(e)
-                scatter(e - 1, 1, y_sb)
-            else:
-                w2_bf = interleave_w2(e)
-                hidden_routed(quantize_w(w_bf1), e, 1, h_bf)
-                hidden_shared(ws_q, 1, range(3, 6))
+            for g in range(2):
+                w1_q[e, g] = quantize_w(*w1_bf[e, g])
+            w2_q[e] = quantize_w(*w2_bf[e])
+        for i, (g, a, b) in enumerate(last_parts):
+            quantize(last_q[g], slice(a, b), last_bf[i][:])
 
-        blocks = ((512, 768), (0, 512))
+        for g in range(2):
+            hidden_shared(w1_q[SHARED, g], g)
+        y_sb = []
+        for e in range(E):
+            h_bf = new_h()
+            for g in range(2):
+                hidden_routed(w1_q[e, g], e, g, h_bf)
+            y_sb.append(second_layer(e, h_bf, w2_q[e]))
+        for e in range(E):
+            for h in range(2):
+                scatter(e, h, y_sb[e])
+        for g in range(2):
+            quantize_shared(g)
+
+        blocks = ((0, 512), (512, 768))
         banks = {}
         for h in range(2):
             for a, b in blocks:
                 banks[h, a] = psum.tile([P, b - a], F32, name="bank", tag="bank")
-
-        last_bf = [held.tile([P, 1024], BF16, name=f"last_bf{g}", align_bytes=64) for g in range(2)]
-        last_q = [held_codes(N, f"last{g}") for g in range(2)]
-
-        def interleave_last(g):
-            rows = raw2[SHARED, g][:].rearrange("p (j n) -> p j n", j=PACK)
-            cut = V_LAST[g]
-            interleave_rows(on_vector, last_bf[g][:, 0 : PACK * cut], rows[:, :, 0:cut])
-            interleave_rows(on_scalar, last_bf[g][:, PACK * cut : PACK * N], rows[:, :, cut:N])
-
-        def multiply_last(g):
+        for g in range(2):
             for h in range(2):
                 for a, b in blocks:
                     multiply(banks[h, a][:], last_q[g], h * P, shared_q[g], slice(a, b), g == 0, g == 1)
-
-        interleave_last(0)
-        y_sb = second_layer(E - 1, h_bf, w2_bf)
-        quantize(last_q[0], slice(0, N), last_bf[0][:])
-        interleave_last(1)
-        multiply_last(0)
-        scatter(E - 1, 0, y_sb)
-        quantize(last_q[1], slice(0, N), last_bf[1][:])
-        multiply_last(1)
-        scatter(E - 1, 1, y_sb)
         for h in range(2):
             for a, b in blocks:
                 result = held.tile([P, b - a], F32, name=f"result{h}_{a}")

@@ -4,10 +4,12 @@ import concourse.mybir as mybir
 
 K, T, E, C, H, N = 512, 768, 4, 128, 1024, 256
 S = E * C
+SHARED = E
 FLOPS = 2 * (T + S) * (K * H + H * N)
 
 F32 = mybir.dt.float32
 BF16 = mybir.dt.bfloat16
+I32 = mybir.dt.int32
 U32 = mybir.dt.uint32
 U16 = mybir.dt.uint16
 U8 = mybir.dt.uint8
@@ -18,18 +20,35 @@ GELU = mybir.ActivationFunctionType.Gelu_apprx_tanh
 
 P = 128
 PACK = 4
-SHARED = E
+PASS = P * PACK
+PASSES = H // PASS
+HALVES = N // P
+CHUNK = PACK * PASS
+LIST_ROWS = 16
 
-TOKEN_CUTS = ((0, 256), (256, 768))
-SCALAR, VECTOR, VECTOR_HALVES, SCALAR_HALVES, VECTOR_SCALAR = range(5)
-W1_COPY = {
-    SHARED: (SCALAR, VECTOR_HALVES),
-    0: (VECTOR_HALVES, VECTOR_HALVES),
-    1: (VECTOR_HALVES, SCALAR),
-    2: (VECTOR, SCALAR),
-    3: (VECTOR, SCALAR_HALVES),
+RAW_BUFS = 7
+BF_BUFS = 7
+CODES_BUFS = PASSES * (E + 1) + E
+
+FIRST_TOKENS = 256
+
+W1_PIECES = {
+    SHARED: (("scalar",), ("scalar",)),
+    0: (("vector", "vector"), ("vector", "vector")),
+    1: (("vector", "vector"), ("scalar",)),
+    2: (("vector",), ("scalar",)),
+    3: (("vector",), ("scalar", "scalar")),
 }
-W2_COPY = {0: VECTOR_HALVES, 1: VECTOR_HALVES, 2: VECTOR_HALVES, 3: VECTOR_SCALAR}
+W2_PIECES = {
+    0: ("vector", "vector"),
+    1: ("vector", "scalar"),
+    2: ("vector", "vector"),
+    3: ("vector", "scalar"),
+}
+
+LAST_PARTS = ((0, 0, N), (1, 0, P), (1, P, N))
+
+TOKEN_BLOCKS = ((0, 512), (512, T))
 
 
 def tile_moe_shr_mlp_gelu_kernel(tc, xT, w1, w2, gate, offs, out):
@@ -46,29 +65,32 @@ def tile_moe_shr_mlp_gelu_kernel(tc, xT, w1, w2, gate, offs, out):
         def on_scalar(dst, src):
             nc.scalar.copy(out=dst, in_=src)
 
+        copy_on = {"vector": on_vector, "scalar": on_scalar}
+
         def held_codes(width, name):
             codes = held.tile([P, width], U32, name=name + "_codes", align_bytes=64)
             scales = held.tile([P, width], U8, name=name + "_scales", align_bytes=64)
             return codes, scales
 
-        def quantize(q, cols, values):
-            nc.vector.quantize_mx(out=q[0][:, cols].bitcast(FP8X4), scales=q[1][:, cols], in_=values)
+        def quantize(operand, cols, values):
+            codes, scales = operand
+            nc.vector.quantize_mx(out=codes[:, cols].bitcast(FP8X4), scales=scales[:, cols], in_=values)
 
-        def multiply(bank, w_q, w_col, x_q, x_cols, start, stop):
-            w_cols = slice(w_col, w_col + P)
+        def multiply(sums, weights, weight_col, moving, moving_cols, start, stop):
+            weight_cols = slice(weight_col, weight_col + P)
             nc.tensor.matmul_mx(
-                out=bank,
-                lhsT=w_q[0][:, w_cols].bitcast(FP8X4),
-                lhsT_scale=w_q[1][:, w_cols],
-                rhs=x_q[0][:, x_cols].bitcast(FP8X4),
-                rhs_scale=x_q[1][:, x_cols],
+                out=sums,
+                lhsT=weights[0][:, weight_cols].bitcast(FP8X4),
+                lhsT_scale=weights[1][:, weight_cols],
+                rhs=moving[0][:, moving_cols].bitcast(FP8X4),
+                rhs_scale=moving[1][:, moving_cols],
                 start=start,
                 stop=stop,
             )
 
         x_rows = xT.rearrange("(p j) t -> p j t", j=PACK)
         x_raw = []
-        offsets = held.tile([P, S // 16], U16, name="offsets")
+        offsets = held.tile([P, S // LIST_ROWS], U16, name="offsets")
 
         def load_tokens(a, b):
             piece = held.tile([P, PACK, b - a], F32, name=f"x_raw{a}")
@@ -78,227 +100,201 @@ def tile_moe_shr_mlp_gelu_kernel(tc, xT, w1, w2, gate, offs, out):
         gates = held.tile([P, S], F32, name="gates")
 
         def load_w1(e, g):
-            raw = work.tile([P, 2048], F32, name="raw", tag="raw", bufs=7)
+            raw = work.tile([P, CHUNK], F32, name="raw", tag="raw", bufs=RAW_BUFS)
             nc.sync.dma_start(
                 out=raw[:].rearrange("p (j c) -> p j c", j=PACK),
-                in_=w1[e].rearrange("(p j) c -> p j c", j=PACK)[:, :, g * 512 : (g + 1) * 512],
+                in_=w1[e].rearrange("(p j) c -> p j c", j=PACK)[:, :, g * PASS : (g + 1) * PASS],
             )
             return raw
 
-        raw1 = {}
-        raw2 = {}
-        load_tokens(0, 256)
+        w1_raw = {}
+        w2_raw = {}
+        load_tokens(0, FIRST_TOKENS)
         nc.sync.dma_start(offsets[:], offs)
-        load_tokens(256, 768)
-        raw1[SHARED, 0] = load_w1(SHARED, 0)
-        raw1[SHARED, 1] = load_w1(SHARED, 1)
+        load_tokens(FIRST_TOKENS, T)
+        w1_raw[SHARED, 0] = load_w1(SHARED, 0)
+        w1_raw[SHARED, 1] = load_w1(SHARED, 1)
         for e in range(E):
-            for g in range(2):
-                raw1[e, g] = load_w1(e, g)
+            for g in range(PASSES):
+                w1_raw[e, g] = load_w1(e, g)
             if e == 0:
                 nc.sync.dma_start(out=gates[:], in_=gate[0:P, :])
-            raw = work.tile([P, 2048], F32, name="raw", tag="raw", bufs=7)
+            raw = work.tile([P, CHUNK], F32, name="raw", tag="raw", bufs=RAW_BUFS)
             nc.sync.dma_start(
-                out=raw[:].rearrange("p (g j n) -> p g j n", g=2, j=PACK),
-                in_=w2[e].rearrange("(g p j) n -> p g j n", g=2, j=PACK),
+                out=raw[:].rearrange("p (g j n) -> p g j n", g=PASSES, j=PACK),
+                in_=w2[e].rearrange("(g p j) n -> p g j n", g=PASSES, j=PACK),
             )
-            raw2[e] = raw
-        last_rows = w2[SHARED].rearrange("(g p j) n -> p g j n", g=2, j=PACK)
-        last_parts = ((0, 0, N), (1, 0, P), (1, P, N))
+            w2_raw[e] = raw
+        last_rows = w2[SHARED].rearrange("(g p j) n -> p g j n", g=PASSES, j=PACK)
         last_raw = []
-        for g, a, b in last_parts:
-            last = held.tile([P, PACK, b - a], F32, name=f"last_raw{g}_{a}")
-            nc.sync.dma_start(out=last[:], in_=last_rows[:, g, :, a:b])
-            last_raw.append(last)
+        for g, a, b in LAST_PARTS:
+            raw = held.tile([P, PACK, b - a], F32, name=f"last_raw{g}_{a}")
+            nc.sync.dma_start(out=raw[:], in_=last_rows[:, g, :, a:b])
+            last_raw.append(raw)
 
         warm = held.tile([P, 1], F32, name="warm")
         nc.gpsimd.memset(warm[:], 0.0)
         warm_out = held.tile([P, 1], F32, name="warm_out")
         nc.scalar.activation(out=warm_out[:], in_=warm[:], func=GELU)
+
         routed = []
-        for h in range(2):
-            window = held.tile([P, T], F32, name=f"routed{h}")
+        for half in range(HALVES):
+            window = held.tile([P, T], F32, name=f"routed{half}")
             nc.gpsimd.memset(window[:], 0.0)
             routed.append(window)
 
-        pairs = [held.tile([P, 2 * T], BF16, name=f"pairs{u}", align_bytes=64) for u in range(2)]
-        x_bf = held.tile([P, PACK * T], BF16, name="x_bf", align_bytes=64)
-        x_q = held_codes(T, "x")
+        pairs = held.tile([P, 2, 2 * T], BF16, name="pairs", align_bytes=64)
+        tokens_bf = held.tile([P, PACK * T], BF16, name="tokens_bf", align_bytes=64)
+        tokens_q = held_codes(T, "token")
         slots_bf = held.tile([P, PACK * S], BF16, name="slots_bf", align_bytes=64)
         slots_q = held_codes(S, "slot")
 
-        def pair_plane(copy, piece, u, a, b):
+        def make_pairs(copy, piece, u, a, b):
             copy(
-                pairs[u][:, 2 * a : 2 * b].rearrange("p (c i k) -> p c k i", i=4, k=2),
-                piece[:, 2 * u : 2 * u + 2, :].rearrange("p k (c i) -> p c k i", i=4),
+                pairs[:, u, 2 * a : 2 * b].rearrange("p (c r k) -> p c k r", r=4, k=2),
+                piece[:, 2 * u : 2 * u + 2, :].rearrange("p k (c r) -> p c k r", r=4),
             )
 
-        def interleave_tokens(copy, piece, a, b):
-            copy(
-                x_bf[:, PACK * a : PACK * b].rearrange("p (c i j) -> p c j i", i=4, j=PACK),
-                piece.rearrange("p j (c i) -> p c j i", i=4),
+        def join_pairs(a, b):
+            nc.vector.tensor_copy(
+                tokens_bf[:, PACK * a : PACK * b].bitcast(I32).rearrange("p (t u) -> p t u", u=2),
+                pairs[:, :, 2 * a : 2 * b].bitcast(I32).rearrange("p u t -> p t u"),
             )
 
-        def gather(u):
+        def gather_pairs(u):
             nc.vector.tensor_copy(
                 slots_bf[:].bitcast(U32).rearrange("p (s u) -> p s u", u=2)[:, :, u],
-                pairs[u][:].bitcast(U32).indirect(offsets[:]),
+                pairs[:, u, :].bitcast(U32).indirect(offsets[:]),
             )
-
-        def engines(choice):
-            return {
-                VECTOR: (on_vector,),
-                SCALAR: (on_scalar,),
-                VECTOR_HALVES: (on_vector, on_vector),
-                SCALAR_HALVES: (on_scalar, on_scalar),
-                VECTOR_SCALAR: (on_vector, on_scalar),
-            }[choice]
-
-        def quantize_w(w_bf, parts):
-            codes = work.tile([P, 512], U32, name="w_codes", tag="w_codes", bufs=14, align_bytes=64)
-            scales = work.tile([P, 512], U8, name="w_scales", tag="w_scales", bufs=14, align_bytes=64)
-            step = 512 // parts
-            for i in range(parts):
-                quantize((codes, scales), slice(i * step, (i + 1) * step), w_bf[:, PACK * i * step : PACK * (i + 1) * step])
-            return codes, scales
 
         def interleave_w1(e, g):
-            w_bf = work.tile([P, 2048], BF16, name="w_bf", tag="w_bf", bufs=7, align_bytes=64)
-            dst = w_bf[:].rearrange("p (t m j) -> p m j t", t=4, j=PACK)
-            src = raw1[e, g][:].rearrange("p (j m t) -> p m j t", j=PACK, t=4)
-            copies = engines(W1_COPY[e][g])
-            step = 4 // len(copies)
-            for i, copy in enumerate(copies):
-                t = slice(i * step, (i + 1) * step)
-                copy(dst[:, :, :, t], src[:, :, :, t])
-            return w_bf, len(copies)
+            w_bf = work.tile([P, CHUNK], BF16, name="w_bf", tag="w_bf", bufs=BF_BUFS, align_bytes=64)
+            dst = w_bf[:].rearrange("p (t m j) -> p m j t", t=PACK, j=PACK)
+            src = w1_raw[e, g][:].rearrange("p (j m t) -> p m j t", j=PACK, t=PACK)
+            pieces = W1_PIECES[e][g]
+            step = PACK // len(pieces)
+            for index, engine in enumerate(pieces):
+                tiles = slice(index * step, (index + 1) * step)
+                copy_on[engine](dst[:, :, :, tiles], src[:, :, :, tiles])
+            return w_bf, len(pieces)
 
-        def interleave_rows(copy, w_bf, raw):
-            copy(
-                w_bf.rearrange("p (c i j) -> p c j i", i=4, j=PACK),
-                raw.rearrange("p j (c i) -> p c j i", i=4),
-            )
+        def interleave_rows(copy, dst, src):
+            copy(dst.rearrange("p (c r j) -> p c j r", r=4, j=PACK), src.rearrange("p j (c r) -> p c j r", r=4))
 
         def interleave_w2(e):
-            w_bf = work.tile([P, 2048], BF16, name="w_bf", tag="w_bf", bufs=7, align_bytes=64)
-            rows = raw2[e][:].rearrange("p (g j n) -> p g j n", g=2, j=PACK)
-            copies = engines(W2_COPY[e])
-            for i, copy in enumerate(copies):
-                interleave_rows(copy, w_bf[:, 1024 * i : 1024 * (i + 1)], rows[:, i])
-            return w_bf, len(copies)
+            w_bf = work.tile([P, CHUNK], BF16, name="w_bf", tag="w_bf", bufs=BF_BUFS, align_bytes=64)
+            rows = w2_raw[e][:].rearrange("p (g j n) -> p g j n", g=PASSES, j=PACK)
+            for g, engine in enumerate(W2_PIECES[e]):
+                interleave_rows(copy_on[engine], w_bf[:, g * PACK * N : (g + 1) * PACK * N], rows[:, g])
+            return w_bf, PASSES
 
-        def hidden(w_q, x, x_col, h_bf):
-            bank = psum.tile([P, 4, P], F32, name="bank", tag="bank")
-            for t in range(4):
-                multiply(bank[:, t, :], w_q, t * P, x, slice(x_col, x_col + P), True, True)
+        def quantize_weights(w_bf, pieces):
+            codes = work.tile([P, PASS], U32, name="w_codes", tag="w_codes", bufs=CODES_BUFS, align_bytes=64)
+            scales = work.tile([P, PASS], U8, name="w_scales", tag="w_scales", bufs=CODES_BUFS, align_bytes=64)
+            step = PASS // pieces
+            for index in range(pieces):
+                a, b = index * step, (index + 1) * step
+                quantize((codes, scales), slice(a, b), w_bf[:, PACK * a : PACK * b])
+            return codes, scales
+
+        def hidden(weights, moving, first, h_bf):
+            bank = psum.tile([P, PACK, P], F32, name="bank", tag="bank")
+            for t in range(PACK):
+                multiply(bank[:, t, :], weights, t * P, moving, slice(first, first + P), True, True)
             nc.scalar.activation(
-                out=h_bf.rearrange("p (n t) -> p n t", t=4),
-                in_=bank[:].rearrange("p t n -> p n t"),
+                out=h_bf.rearrange("p (c t) -> p c t", t=PACK),
+                in_=bank[:].rearrange("p t c -> p c t"),
                 func=GELU,
             )
 
-        shared_bf = [held.tile([P, PACK * T], BF16, name=f"hs_bf{g}", align_bytes=64) for g in range(2)]
-        shared_q = [held_codes(T, f"hs{g}") for g in range(2)]
+        hs_bf = [held.tile([P, PACK * T], BF16, name=f"hs_bf{g}", align_bytes=64) for g in range(PASSES)]
+        hs_q = [held_codes(T, f"hs{g}") for g in range(PASSES)]
 
-        def hidden_shared(w_q, g):
-            for b in range(T // P):
-                hidden(w_q, x_q, b * P, shared_bf[g][:, b * 512 : (b + 1) * 512])
+        def hidden_shared(weights, g):
+            for first in range(0, T, P):
+                hidden(weights, tokens_q, first, hs_bf[g][:, PACK * first : PACK * (first + P)])
 
-        def quantize_shared(g):
-            quantize(shared_q[g], slice(0, 512), shared_bf[g][:, 0:2048])
-            quantize(shared_q[g], slice(512, 768), shared_bf[g][:, 2048:3072])
-
-        def hidden_routed(w_q, e, g, h_bf):
-            hidden(w_q, slots_q, e * C, h_bf[:, g * 512 : (g + 1) * 512])
-
-        def new_h():
-            return work.tile([P, H], BF16, name="h_bf", tag="h_bf", bufs=4, align_bytes=64)
-
-        def second_layer(e, h_bf, w2_q):
-            h_codes = work.tile([P, 2 * C], U32, name="h_codes", tag="h_codes", bufs=4, align_bytes=64)
-            h_scales = work.tile([P, 2 * C], U8, name="h_scales", tag="h_scales", bufs=4, align_bytes=64)
+        def second_layer(e, h_bf, weights):
+            h_codes = work.tile([P, PASSES * C], U32, name="h_codes", tag="h_codes", bufs=E, align_bytes=64)
+            h_scales = work.tile([P, PASSES * C], U8, name="h_scales", tag="h_scales", bufs=E, align_bytes=64)
             h_q = (h_codes, h_scales)
-            quantize(h_q, slice(0, 2 * C), h_bf[:])
-            y = psum.tile([P, 2, C], F32, name="bank", tag="bank")
-            for h in range(2):
-                for g in range(2):
-                    multiply(y[:, h, :], w2_q, g * N + h * P, h_q, slice(g * C, (g + 1) * C), g == 0, g == 1)
-            y_sb = work.tile([P, 2, C], F32, name="y_sb", tag="y_sb", bufs=4)
-            for h in range(2):
-                nc.vector.tensor_tensor(y_sb[:, h, :], y[:, h, :], gates[:, e * C : (e + 1) * C], MULT)
-            return y_sb
+            quantize(h_q, slice(0, PASSES * C), h_bf[:])
+            y = psum.tile([P, HALVES, C], F32, name="bank", tag="bank")
+            for half in range(HALVES):
+                for g in range(PASSES):
+                    start, stop = g == 0, g == PASSES - 1
+                    multiply(y[:, half, :], weights, g * N + half * P, h_q, slice(g * C, (g + 1) * C), start, stop)
+            gated = work.tile([P, HALVES, C], F32, name="gated", tag="gated", bufs=E)
+            for half in range(HALVES):
+                nc.vector.tensor_tensor(gated[:, half, :], y[:, half, :], gates[:, e * C : (e + 1) * C], MULT)
+            return gated
 
-        def scatter(e, h, y_sb):
-            nc.vector.tensor_copy(routed[h][:].indirect(offsets[:, e * C // 16 : (e + 1) * C // 16]), y_sb[:, h, :])
+        def scatter(e, half, gated):
+            list_cols = slice(e * C // LIST_ROWS, (e + 1) * C // LIST_ROWS)
+            nc.vector.tensor_copy(routed[half][:].indirect(offsets[:, list_cols]), gated[:, half, :])
 
-        last_bf = [held.tile([P, PACK * (b - a)], BF16, name=f"last_bf{g}_{a}", align_bytes=64) for g, a, b in last_parts]
-        last_q = [held_codes(N, f"last{g}") for g in range(2)]
+        last_bf = [held.tile([P, PACK * (b - a)], BF16, name=f"last_bf{g}_{a}", align_bytes=64) for g, a, b in LAST_PARTS]
+        last_q = [held_codes(N, f"last{g}") for g in range(PASSES)]
 
-        def interleave_last(i):
-            width = last_raw[i].shape[2]
-            cut = width // 2
-            interleave_rows(on_vector, last_bf[i][:, 0 : PACK * cut], last_raw[i][:, :, 0:cut])
-            interleave_rows(on_scalar, last_bf[i][:, PACK * cut : PACK * width], last_raw[i][:, :, cut:width])
-
-        pair_plane(on_vector, x_raw[0][:], 0, 0, 256)
-        pair_plane(on_scalar, x_raw[0][:], 1, 0, 256)
-        interleave_tokens(on_scalar, x_raw[0][:], 0, 256)
-        pair_plane(on_vector, x_raw[1][:], 0, 256, 768)
-        pair_plane(on_scalar, x_raw[1][:], 1, 256, 768)
-        interleave_tokens(on_vector, x_raw[1][:, :, 0:256], 256, 512)
-        interleave_tokens(on_scalar, x_raw[1][:, :, 256:512], 512, 768)
+        for piece, a, b in ((x_raw[0], 0, FIRST_TOKENS), (x_raw[1], FIRST_TOKENS, T)):
+            make_pairs(on_vector, piece[:], 0, a, b)
+            make_pairs(on_scalar, piece[:], 1, a, b)
+            join_pairs(a, b)
 
         w1_bf = {}
         w2_bf = {}
         for e in [SHARED] + list(range(E)):
-            for g in range(2):
+            for g in range(PASSES):
                 w1_bf[e, g] = interleave_w1(e, g)
             if e != SHARED:
                 w2_bf[e] = interleave_w2(e)
-        for i in range(3):
-            interleave_last(i)
+        for raw, w_bf in zip(last_raw, last_bf):
+            cut = raw.shape[2] // 2
+            interleave_rows(on_vector, w_bf[:, : PACK * cut], raw[:, :, :cut])
+            interleave_rows(on_scalar, w_bf[:, PACK * cut :], raw[:, :, cut:])
 
-        quantize(x_q, slice(0, 256), x_bf[:, 0:1024])
-        quantize(x_q, slice(256, 768), x_bf[:, 1024:3072])
+        for a, b in ((0, FIRST_TOKENS), (FIRST_TOKENS, T)):
+            quantize(tokens_q, slice(a, b), tokens_bf[:, PACK * a : PACK * b])
         w1_q = {}
         w2_q = {}
-        w1_q[SHARED, 0] = quantize_w(*w1_bf[SHARED, 0])
-        gather(0)
-        gather(1)
-        w1_q[SHARED, 1] = quantize_w(*w1_bf[SHARED, 1])
+        w1_q[SHARED, 0] = quantize_weights(*w1_bf[SHARED, 0])
+        gather_pairs(0)
+        gather_pairs(1)
+        w1_q[SHARED, 1] = quantize_weights(*w1_bf[SHARED, 1])
         quantize(slots_q, slice(0, S), slots_bf[:])
         for e in range(E):
-            for g in range(2):
-                w1_q[e, g] = quantize_w(*w1_bf[e, g])
-            w2_q[e] = quantize_w(*w2_bf[e])
-        for i, (g, a, b) in enumerate(last_parts):
-            quantize(last_q[g], slice(a, b), last_bf[i][:])
+            for g in range(PASSES):
+                w1_q[e, g] = quantize_weights(*w1_bf[e, g])
+            w2_q[e] = quantize_weights(*w2_bf[e])
+        for (g, a, b), w_bf in zip(LAST_PARTS, last_bf):
+            quantize(last_q[g], slice(a, b), w_bf[:])
 
-        for g in range(2):
+        for g in range(PASSES):
             hidden_shared(w1_q[SHARED, g], g)
-        y_sb = []
+        gated_by_expert = []
         for e in range(E):
-            h_bf = new_h()
-            for g in range(2):
-                hidden_routed(w1_q[e, g], e, g, h_bf)
-            y_sb.append(second_layer(e, h_bf, w2_q[e]))
+            h_bf = work.tile([P, PACK * PASSES * C], BF16, name="h_bf", tag="h_bf", bufs=E, align_bytes=64)
+            for g in range(PASSES):
+                hidden(w1_q[e, g], slots_q, e * C, h_bf[:, g * PACK * C : (g + 1) * PACK * C])
+            gated_by_expert.append(second_layer(e, h_bf, w2_q[e]))
         for e in range(E):
-            for h in range(2):
-                scatter(e, h, y_sb[e])
-        for g in range(2):
-            quantize_shared(g)
+            for half in range(HALVES):
+                scatter(e, half, gated_by_expert[e])
+        for g in range(PASSES):
+            for a, b in TOKEN_BLOCKS:
+                quantize(hs_q[g], slice(a, b), hs_bf[g][:, PACK * a : PACK * b])
 
-        blocks = ((0, 512), (512, 768))
         banks = {}
-        for h in range(2):
-            for a, b in blocks:
-                banks[h, a] = psum.tile([P, b - a], F32, name="bank", tag="bank")
-        for g in range(2):
-            for h in range(2):
-                for a, b in blocks:
-                    multiply(banks[h, a][:], last_q[g], h * P, shared_q[g], slice(a, b), g == 0, g == 1)
-        for h in range(2):
-            for a, b in blocks:
-                result = held.tile([P, b - a], F32, name=f"result{h}_{a}")
-                nc.vector.tensor_tensor(result[:], banks[h, a][:], routed[h][:, a:b], ADD)
-                nc.sync.dma_start(out=out[h * P : (h + 1) * P, a:b], in_=result[:])
+        for half in range(HALVES):
+            for a, b in TOKEN_BLOCKS:
+                banks[half, a] = psum.tile([P, b - a], F32, name="bank", tag="bank")
+        for g in range(PASSES):
+            for half in range(HALVES):
+                for a, b in TOKEN_BLOCKS:
+                    start, stop = g == 0, g == PASSES - 1
+                    multiply(banks[half, a][:], last_q[g], half * P, hs_q[g], slice(a, b), start, stop)
+        for half in range(HALVES):
+            for a, b in TOKEN_BLOCKS:
+                result = held.tile([P, b - a], F32, name=f"result{half}_{a}")
+                nc.vector.tensor_tensor(result[:], banks[half, a][:], routed[half][:, a:b], ADD)
+                nc.sync.dma_start(out=out[half * P : (half + 1) * P, a:b], in_=result[:])

from contextlib import ExitStack

import concourse.mybir as mybir

K, T, E, C, H, N = 512, 768, 4, 128, 1024, 256
S = E * C
SHARED = E
FLOPS = 2 * (T + S) * (K * H + H * N)

F32 = mybir.dt.float32
BF16 = mybir.dt.bfloat16
I32 = mybir.dt.int32
U32 = mybir.dt.uint32
U16 = mybir.dt.uint16
U8 = mybir.dt.uint8
FP8X4 = mybir.dt.float8_e4m3fn_x4
ADD = mybir.AluOpType.add
MULT = mybir.AluOpType.mult
GELU = mybir.ActivationFunctionType.Gelu_apprx_tanh

P = 128
PACK = 4
PASS = P * PACK
PASSES = H // PASS
HALVES = N // P
CHUNK = PACK * PASS
LIST_ROWS = 16

RAW_BUFS = 7
BF_BUFS = 7
CODES_BUFS = PASSES * (E + 1) + E

FIRST_TOKENS = 256

W1_PIECES = {
    SHARED: (("scalar",), ("scalar",)),
    0: (("vector", "vector"), ("vector", "vector")),
    1: (("vector", "vector"), ("scalar",)),
    2: (("vector",), ("scalar",)),
    3: (("vector",), ("scalar", "scalar")),
}
W2_PIECES = {
    0: ("vector", "vector"),
    1: ("vector", "scalar"),
    2: ("vector", "vector"),
    3: ("vector", "scalar"),
}

LAST_PARTS = ((0, 0, N), (1, 0, P), (1, P, N))

TOKEN_BLOCKS = ((0, 512), (512, T))


def tile_moe_shr_mlp_gelu_kernel(tc, xT, w1, w2, gate, offs, out):
    nc = tc.nc

    with ExitStack() as ctx:
        held = ctx.enter_context(tc.tile_pool(name="held", bufs=1))
        work = ctx.enter_context(tc.tile_pool(name="work", bufs=2))
        psum = ctx.enter_context(tc.psum_pool(name="psum", bufs=8))

        def on_vector(dst, src):
            nc.vector.tensor_copy(out=dst, in_=src)

        def on_scalar(dst, src):
            nc.scalar.copy(out=dst, in_=src)

        copy_on = {"vector": on_vector, "scalar": on_scalar}

        def held_codes(width, name):
            codes = held.tile([P, width], U32, name=name + "_codes", align_bytes=64)
            scales = held.tile([P, width], U8, name=name + "_scales", align_bytes=64)
            return codes, scales

        def quantize(operand, cols, values):
            codes, scales = operand
            nc.vector.quantize_mx(out=codes[:, cols].bitcast(FP8X4), scales=scales[:, cols], in_=values)

        def multiply(sums, weights, weight_col, moving, moving_cols, start, stop):
            weight_cols = slice(weight_col, weight_col + P)
            nc.tensor.matmul_mx(
                out=sums,
                lhsT=weights[0][:, weight_cols].bitcast(FP8X4),
                lhsT_scale=weights[1][:, weight_cols],
                rhs=moving[0][:, moving_cols].bitcast(FP8X4),
                rhs_scale=moving[1][:, moving_cols],
                start=start,
                stop=stop,
            )

        x_rows = xT.rearrange("(p j) t -> p j t", j=PACK)
        x_raw = []
        offsets = held.tile([P, S // LIST_ROWS], U16, name="offsets")

        def load_tokens(a, b):
            piece = held.tile([P, PACK, b - a], F32, name=f"x_raw{a}")
            nc.sync.dma_start(out=piece[:], in_=x_rows[:, :, a:b])
            x_raw.append(piece)

        gates = held.tile([P, S], F32, name="gates")

        def load_w1(e, g):
            raw = work.tile([P, CHUNK], F32, name="raw", tag="raw", bufs=RAW_BUFS)
            nc.sync.dma_start(
                out=raw[:].rearrange("p (j c) -> p j c", j=PACK),
                in_=w1[e].rearrange("(p j) c -> p j c", j=PACK)[:, :, g * PASS : (g + 1) * PASS],
            )
            return raw

        w1_raw = {}
        w2_raw = {}
        load_tokens(0, FIRST_TOKENS)
        nc.sync.dma_start(offsets[:], offs)
        load_tokens(FIRST_TOKENS, T)
        w1_raw[SHARED, 0] = load_w1(SHARED, 0)
        w1_raw[SHARED, 1] = load_w1(SHARED, 1)
        for e in range(E):
            for g in range(PASSES):
                w1_raw[e, g] = load_w1(e, g)
            if e == 0:
                nc.sync.dma_start(out=gates[:], in_=gate[0:P, :])
            raw = work.tile([P, CHUNK], F32, name="raw", tag="raw", bufs=RAW_BUFS)
            nc.sync.dma_start(
                out=raw[:].rearrange("p (g j n) -> p g j n", g=PASSES, j=PACK),
                in_=w2[e].rearrange("(g p j) n -> p g j n", g=PASSES, j=PACK),
            )
            w2_raw[e] = raw
        last_rows = w2[SHARED].rearrange("(g p j) n -> p g j n", g=PASSES, j=PACK)
        last_raw = []
        for g, a, b in LAST_PARTS:
            raw = held.tile([P, PACK, b - a], F32, name=f"last_raw{g}_{a}")
            nc.sync.dma_start(out=raw[:], in_=last_rows[:, g, :, a:b])
            last_raw.append(raw)

        warm = held.tile([P, 1], F32, name="warm")
        nc.gpsimd.memset(warm[:], 0.0)
        warm_out = held.tile([P, 1], F32, name="warm_out")
        nc.scalar.activation(out=warm_out[:], in_=warm[:], func=GELU)

        routed = []
        for half in range(HALVES):
            window = held.tile([P, T], F32, name=f"routed{half}")
            nc.gpsimd.memset(window[:], 0.0)
            routed.append(window)

        pairs = held.tile([P, 2, 2 * T], BF16, name="pairs", align_bytes=64)
        tokens_bf = held.tile([P, PACK * T], BF16, name="tokens_bf", align_bytes=64)
        tokens_q = held_codes(T, "token")
        slots_bf = held.tile([P, PACK * S], BF16, name="slots_bf", align_bytes=64)
        slots_q = held_codes(S, "slot")

        def make_pairs(copy, piece, u, a, b):
            copy(
                pairs[:, u, 2 * a : 2 * b].rearrange("p (c r k) -> p c k r", r=4, k=2),
                piece[:, 2 * u : 2 * u + 2, :].rearrange("p k (c r) -> p c k r", r=4),
            )

        def join_pairs(a, b):
            nc.vector.tensor_copy(
                tokens_bf[:, PACK * a : PACK * b].bitcast(I32).rearrange("p (t u) -> p t u", u=2),
                pairs[:, :, 2 * a : 2 * b].bitcast(I32).rearrange("p u t -> p t u"),
            )

        def gather_pairs(u):
            nc.vector.tensor_copy(
                slots_bf[:].bitcast(U32).rearrange("p (s u) -> p s u", u=2)[:, :, u],
                pairs[:, u, :].bitcast(U32).indirect(offsets[:]),
            )

        def interleave_w1(e, g):
            w_bf = work.tile([P, CHUNK], BF16, name="w_bf", tag="w_bf", bufs=BF_BUFS, align_bytes=64)
            dst = w_bf[:].rearrange("p (t m j) -> p m j t", t=PACK, j=PACK)
            src = w1_raw[e, g][:].rearrange("p (j m t) -> p m j t", j=PACK, t=PACK)
            pieces = W1_PIECES[e][g]
            step = PACK // len(pieces)
            for index, engine in enumerate(pieces):
                tiles = slice(index * step, (index + 1) * step)
                copy_on[engine](dst[:, :, :, tiles], src[:, :, :, tiles])
            return w_bf, len(pieces)

        def interleave_rows(copy, dst, src):
            copy(dst.rearrange("p (c r j) -> p c j r", r=4, j=PACK), src.rearrange("p j (c r) -> p c j r", r=4))

        def interleave_w2(e):
            w_bf = work.tile([P, CHUNK], BF16, name="w_bf", tag="w_bf", bufs=BF_BUFS, align_bytes=64)
            rows = w2_raw[e][:].rearrange("p (g j n) -> p g j n", g=PASSES, j=PACK)
            for g, engine in enumerate(W2_PIECES[e]):
                interleave_rows(copy_on[engine], w_bf[:, g * PACK * N : (g + 1) * PACK * N], rows[:, g])
            return w_bf, PASSES

        def quantize_weights(w_bf, pieces):
            codes = work.tile([P, PASS], U32, name="w_codes", tag="w_codes", bufs=CODES_BUFS, align_bytes=64)
            scales = work.tile([P, PASS], U8, name="w_scales", tag="w_scales", bufs=CODES_BUFS, align_bytes=64)
            step = PASS // pieces
            for index in range(pieces):
                a, b = index * step, (index + 1) * step
                quantize((codes, scales), slice(a, b), w_bf[:, PACK * a : PACK * b])
            return codes, scales

        def hidden(weights, moving, first, h_bf):
            bank = psum.tile([P, PACK, P], F32, name="bank", tag="bank")
            for t in range(PACK):
                multiply(bank[:, t, :], weights, t * P, moving, slice(first, first + P), True, True)
            nc.scalar.activation(
                out=h_bf.rearrange("p (c t) -> p c t", t=PACK),
                in_=bank[:].rearrange("p t c -> p c t"),
                func=GELU,
            )

        hs_bf = [held.tile([P, PACK * T], BF16, name=f"hs_bf{g}", align_bytes=64) for g in range(PASSES)]
        hs_q = [held_codes(T, f"hs{g}") for g in range(PASSES)]

        def hidden_shared(weights, g):
            for first in range(0, T, P):
                hidden(weights, tokens_q, first, hs_bf[g][:, PACK * first : PACK * (first + P)])

        def second_layer(e, h_bf, weights):
            h_codes = work.tile([P, PASSES * C], U32, name="h_codes", tag="h_codes", bufs=E, align_bytes=64)
            h_scales = work.tile([P, PASSES * C], U8, name="h_scales", tag="h_scales", bufs=E, align_bytes=64)
            h_q = (h_codes, h_scales)
            quantize(h_q, slice(0, PASSES * C), h_bf[:])
            y = psum.tile([P, HALVES, C], F32, name="bank", tag="bank")
            for half in range(HALVES):
                for g in range(PASSES):
                    start, stop = g == 0, g == PASSES - 1
                    multiply(y[:, half, :], weights, g * N + half * P, h_q, slice(g * C, (g + 1) * C), start, stop)
            gated = work.tile([P, HALVES, C], F32, name="gated", tag="gated", bufs=E)
            for half in range(HALVES):
                nc.vector.tensor_tensor(gated[:, half, :], y[:, half, :], gates[:, e * C : (e + 1) * C], MULT)
            return gated

        def scatter(e, half, gated):
            list_cols = slice(e * C // LIST_ROWS, (e + 1) * C // LIST_ROWS)
            nc.vector.tensor_copy(routed[half][:].indirect(offsets[:, list_cols]), gated[:, half, :])

        last_bf = [held.tile([P, PACK * (b - a)], BF16, name=f"last_bf{g}_{a}", align_bytes=64) for g, a, b in LAST_PARTS]
        last_q = [held_codes(N, f"last{g}") for g in range(PASSES)]

        for piece, a, b in ((x_raw[0], 0, FIRST_TOKENS), (x_raw[1], FIRST_TOKENS, T)):
            make_pairs(on_vector, piece[:], 0, a, b)
            make_pairs(on_scalar, piece[:], 1, a, b)
            join_pairs(a, b)

        w1_bf = {}
        w2_bf = {}
        for e in [SHARED] + list(range(E)):
            for g in range(PASSES):
                w1_bf[e, g] = interleave_w1(e, g)
            if e != SHARED:
                w2_bf[e] = interleave_w2(e)
        for raw, w_bf in zip(last_raw, last_bf):
            cut = raw.shape[2] // 2
            interleave_rows(on_vector, w_bf[:, : PACK * cut], raw[:, :, :cut])
            interleave_rows(on_scalar, w_bf[:, PACK * cut :], raw[:, :, cut:])

        for a, b in ((0, FIRST_TOKENS), (FIRST_TOKENS, T)):
            quantize(tokens_q, slice(a, b), tokens_bf[:, PACK * a : PACK * b])
        w1_q = {}
        w2_q = {}
        w1_q[SHARED, 0] = quantize_weights(*w1_bf[SHARED, 0])
        gather_pairs(0)
        gather_pairs(1)
        w1_q[SHARED, 1] = quantize_weights(*w1_bf[SHARED, 1])
        quantize(slots_q, slice(0, S), slots_bf[:])
        for e in range(E):
            for g in range(PASSES):
                w1_q[e, g] = quantize_weights(*w1_bf[e, g])
            w2_q[e] = quantize_weights(*w2_bf[e])
        for (g, a, b), w_bf in zip(LAST_PARTS, last_bf):
            quantize(last_q[g], slice(a, b), w_bf[:])

        for g in range(PASSES):
            hidden_shared(w1_q[SHARED, g], g)
        gated_by_expert = []
        for e in range(E):
            h_bf = work.tile([P, PACK * PASSES * C], BF16, name="h_bf", tag="h_bf", bufs=E, align_bytes=64)
            for g in range(PASSES):
                hidden(w1_q[e, g], slots_q, e * C, h_bf[:, g * PACK * C : (g + 1) * PACK * C])
            gated_by_expert.append(second_layer(e, h_bf, w2_q[e]))
        for e in range(E):
            for half in range(HALVES):
                scatter(e, half, gated_by_expert[e])
        for g in range(PASSES):
            for a, b in TOKEN_BLOCKS:
                quantize(hs_q[g], slice(a, b), hs_bf[g][:, PACK * a : PACK * b])

        banks = {}
        for half in range(HALVES):
            for a, b in TOKEN_BLOCKS:
                banks[half, a] = psum.tile([P, b - a], F32, name="bank", tag="bank")
        for g in range(PASSES):
            for half in range(HALVES):
                for a, b in TOKEN_BLOCKS:
                    start, stop = g == 0, g == PASSES - 1
                    multiply(banks[half, a][:], last_q[g], half * P, hs_q[g], slice(a, b), start, stop)
        for half in range(HALVES):
            for a, b in TOKEN_BLOCKS:
                result = held.tile([P, b - a], F32, name=f"result{half}_{a}")
                nc.vector.tensor_tensor(result[:], banks[half, a][:], routed[half][:, a:b], ADD)
                nc.sync.dma_start(out=out[half * P : (half + 1) * P, a:b], in_=result[:])
